import numpy as np
import ml_dtypes


def mxq(x, axis, fmt="e4m3"):
    dtype, down = {"e4m3": (ml_dtypes.float8_e4m3fn, 7), "e5m2": (ml_dtypes.float8_e5m2, 14)}[fmt]
    v = np.moveaxis(np.asarray(x, np.float32).astype(ml_dtypes.bfloat16).astype(np.float64), axis, -1)
    blocks = v.reshape(v.shape[:-1] + (-1, 32))
    amax = np.abs(blocks).max(-1, keepdims=True)
    byte = np.maximum(np.where(amax > 0, np.frexp(amax)[1] - 1 + 127, 0) - down, 1)
    scale = np.exp2(byte - 127.0)
    codes = (blocks / scale).astype(np.float32).astype(dtype).astype(np.float64)
    return np.moveaxis((codes * scale).reshape(v.shape), -1, axis)


WIDE = False


def mx_kscale(k):
    if not WIDE:
        return np.ones(k)
    levels = np.array([10, -10, 5, -5, 0])
    if k % 512:
        return np.exp2(np.random.permutation(np.resize(levels, k // 32))).repeat(32)
    a = np.empty((k // 512, 16))
    for p in range(k // 512):
        a[p, :8] = np.random.permutation(np.resize(levels, 8))
        for g in range(8):
            far = levels[np.abs(levels - a[p, g]) >= 10]
            a[p, g + 8] = far[np.random.randint(len(far))]
    return np.exp2(a.ravel()).repeat(32)


BF16 = ml_dtypes.bfloat16


def bf(x):
    return np.asarray(x, np.float32).astype(BF16)


def f64(x):
    return np.asarray(x).astype(np.float64)


E2M1 = np.array([0.0, 0.5, 1.0, 1.5, 2.0, 3.0, 4.0, 6.0, -0.0, -0.5, -1.0, -1.5, -2.0, -3.0, -4.0, -6.0])


def pack_weight(w, fmt):
    k, n = w.shape
    w = f64(bf(w)).reshape(k // 32, 32, n)
    amax = np.abs(w).max(1)
    if fmt == "e4m3":
        byte = np.frexp(amax)[1] - 1 + 127 - 7
    else:
        mant, ex = np.frexp(amax / 6.0)
        byte = np.where(mant > 0.5, ex, ex - 1) + 127
    byte = np.clip(np.where(amax > 0, byte, 1), 1, 254)
    scaled = (w * np.exp2(127.0 - byte)[:, None, :]).reshape(k, n).astype(np.float32)
    by_word = np.ascontiguousarray(scaled.reshape(k // 512, 128, 4, n).transpose(0, 1, 3, 2))
    if fmt == "e4m3":
        words = by_word.astype(ml_dtypes.float8_e4m3fn).view(np.uint8)
    else:
        c = by_word.astype(ml_dtypes.float4_e2m1fn).view(np.uint8) & 0xF
        words = c[..., 0::2] | (c[..., 1::2] << 4)
    return np.ascontiguousarray(words), np.ascontiguousarray(byte.astype(np.uint8).reshape(k // 512, 16, n))


def unpack_weight(words, scales, fmt):
    g, p, n, _ = words.shape
    if fmt == "e4m3":
        vals = np.ascontiguousarray(words).view(ml_dtypes.float8_e4m3fn).astype(np.float64)
    else:
        nib = np.empty((g, p, n, 4), np.uint8)
        nib[..., 0::2] = words & 0xF
        nib[..., 1::2] = words >> 4
        vals = E2M1[nib]
    vals = vals * np.repeat(np.exp2(scales.astype(np.float64) - 127.0), 8, axis=1)[..., None]
    return vals.transpose(0, 1, 3, 2).reshape(g * 512, n)
def pack4(w):
    words, scales = pack_weight(w, "e2m1")
    return words.reshape(words.shape[0], 128, -1), scales


def unpack4(words, scales):
    return unpack_weight(words.reshape(words.shape[0], 128, -1, 2), scales, "e2m1")


def planes(Y):
    n, m = Y.shape
    b = f64(bf(Y)).reshape(n // 32, 32, m)
    amax = np.abs(b).max(1)
    byte = np.clip(np.where(amax > 0, np.frexp(amax)[1] - 1 + 127 - 7, 1), 1, 254)
    codes = (b * np.exp2(127.0 - byte)[:, None, :]).reshape(n, m).astype(np.float32).astype(ml_dtypes.float8_e4m3fn).view(np.uint8)
    words = codes.reshape(n // 512, 128, 4, m).transpose(0, 1, 3, 2)
    return np.ascontiguousarray(words), np.ascontiguousarray(byte.astype(np.uint8).reshape(n // 512, 16, m))


M, K, N = 2048, 1536, 1024

STEEPNESS = 1.5
FRICTION = 0.6


def setup_inputs():
    s = mx_kscale(K)
    force = np.random.randn(K, M) * s[:, None]
    f_words, f_scales = pack_weight(force, "e4m3")
    lever = np.exp(0.8 * np.random.randn(N))
    jac = np.random.randn(K, N) * lever[None, :] / np.sqrt(K) / s[:, None]
    qd = np.random.randn(M, N)
    friction = FRICTION * lever * np.exp(0.2 * np.random.randn(N))
    steep = STEEPNESS * np.exp(0.5 * np.random.randn(N))
    return {"f_words": f_words, "f_scales": f_scales, "jac": bf(jac),
            "qd": bf(qd), "friction": bf(friction), "steep": bf(steep)}


def reference(f_words, f_scales, jac, qd, friction, steep):
    F = unpack_weight(f_words, f_scales, "e4m3")
    tau = F.T @ mxq(f64(jac), 0, "e4m3")
    y = tau - f64(friction) * np.tanh(f64(steep) * f64(qd))
    Y = y.T
    words, scales = planes(Y)
    return y, words, scales

@@ -1,0 +1,287 @@
+from contextlib import ExitStack
+
+import concourse.mybir as mybir
+from concourse.masks import make_identity
+
+M, K, N = 2048, 1536, 1024
+FLOPS = 2 * M * K * N
+
+F32 = mybir.dt.float32
+BF16 = mybir.dt.bfloat16
+I32 = mybir.dt.int32
+U32 = mybir.dt.uint32
+U8 = mybir.dt.uint8
+FP8X4 = mybir.dt.float8_e4m3fn_x4
+ALU = mybir.AluOpType
+ACT = mybir.ActivationFunctionType
+
+P = 128
+PACK = 4
+GROUP = P * PACK
+PASSES = K // GROUP
+GROUPS = N // GROUP
+CHUNK = 512
+CHUNKS = M // CHUNK
+TILES = CHUNK // P
+BANKS = 8
+
+
+def tile_joint_torque_friction_planes_g6_kernel(
+    tc, f_words, f_scales, jac, qd, friction, steep, out_0, out_1, out_2
+):
+    nc = tc.nc
+    units = [(g, c) for g in range(GROUPS) for c in range(CHUNKS)]
+    last = len(units) - 1
+
+    with ExitStack() as ctx:
+        keep = ctx.enter_context(tc.tile_pool(name="keep", bufs=1))
+        work = ctx.enter_context(tc.tile_pool(name="work", bufs=2))
+        stage = ctx.enter_context(tc.tile_pool(name="stage", bufs=4))
+        psum = ctx.enter_context(tc.psum_pool(name="psum", bufs=1))
+        ctx.enter_context(tc.manual_schedule())
+
+        ring = []
+
+        def next_bank():
+            k = len(ring) % BANKS
+            ring.append(k)
+            return psum.tile([P, CHUNK], F32, name="bank%d" % k)
+
+        ident = keep.tile([P, P], F32, name="ident")
+        f_plane = keep.tile([P, M], U8, name="f_plane", align_bytes=64)
+        zero_in = keep.tile([P, 1], F32, name="zero_in")
+        zero_bias = keep.tile([P, 1], F32, name="zero_bias")
+        steep_raw = keep.tile([P, GROUPS, PACK], BF16, name="steep_raw")
+        fric_raw = keep.tile([P, GROUPS, PACK], BF16, name="fric_raw")
+        steep_col = keep.tile([P, GROUPS, PACK], F32, name="steep_col")
+        neg_fric_col = keep.tile([P, GROUPS, PACK], F32, name="neg_fric_col")
+        y_planes = [keep.tile([P, M], U8, name="y_plane%d" % g, align_bytes=64) for g in range(GROUPS)]
+
+        j_raw, j_grouped, j_codes, j_scales = {}, {}, {}, {}
+        f_codes, q_raw, q_banks, tanh_t, tau, y_t, y_banks, y_rows, y_bf, y_codes = ({} for i in range(10))
+
+        f_view = f_words.rearrange("g p m t -> p g (m t)")
+
+        def load_j(kp, g):
+            j_raw[kp, g] = keep.tile([P, PACK, GROUP], BF16, name="j_raw%d_%d" % (kp, g))
+            rows = jac[kp * GROUP : (kp + 1) * GROUP, g * GROUP : (g + 1) * GROUP]
+            nc.sync.dma_start(out=j_raw[kp, g][:], in_=rows.rearrange("(p j) n -> p j n", j=PACK))
+
+        def load_f(c, kps):
+            tile = keep.tile([P, len(kps), CHUNK], U32, name="f_codes%d_%d" % (c, kps[0]), align_bytes=64)
+            src = f_view[:, kps[0] : kps[-1] + 1, PACK * CHUNK * c : PACK * CHUNK * (c + 1)]
+            nc.sync.dma_start(out=tile[:].bitcast(I32), in_=src.bitcast(I32))
+            for i, kp in enumerate(kps):
+                f_codes[kp, c] = tile[:, i, :]
+
+        def load_q(u):
+            g, c = units[u]
+            q_raw[u] = keep.tile([P, TILES, GROUP], BF16, name="q_raw%d" % u)
+            rows = qd[c * CHUNK : (c + 1) * CHUNK, g * GROUP : (g + 1) * GROUP]
+            nc.sync.dma_start(out=q_raw[u][:], in_=rows.rearrange("(i p) n -> p i n", p=P))
+
+        def group_j(kp, g, h):
+            tile = stage.tile([P, 2, P, PACK], BF16, name="j_grouped", align_bytes=64)
+            j_grouped[kp, g, h] = tile
+            src = j_raw[kp, g][:].rearrange("p j (m t) -> p m j t", t=PACK)[:, :, :, 2 * h : 2 * h + 2]
+            dst = tile[:].rearrange("p t m j -> p m j t")
+            if h == 0:
+                nc.vector.tensor_copy(out=dst, in_=src)
+            else:
+                nc.scalar.copy(out=dst, in_=src)
+
+        def quant_j(kp, g, h):
+            codes = keep.tile([P, 2 * P], U32, name="j_codes%d_%d_%d" % (kp, g, h), align_bytes=64)
+            scales = keep.tile([P, 2 * P], U8, name="j_scales%d_%d_%d" % (kp, g, h), align_bytes=64)
+            nc.vector.quantize_mx(
+                out=codes[:].bitcast(FP8X4),
+                scales=scales[:],
+                in_=j_grouped[kp, g, h][:].rearrange("p t m j -> p (t m j)"),
+            )
+            for e in range(2):
+                j_codes[kp, g, 2 * h + e] = codes[:, e * P : (e + 1) * P]
+                j_scales[kp, g, 2 * h + e] = scales[:, e * P : (e + 1) * P]
+
+        def mx_pass(u, t, kp):
+            g, c = units[u]
+            if kp == 0:
+                tau[u, t] = next_bank()
+            nc.tensor.matmul_mx(
+                out=tau[u, t][:],
+                lhsT=j_codes[kp, g, t].bitcast(FP8X4),
+                lhsT_scale=j_scales[kp, g, t],
+                rhs=f_codes[kp, c].bitcast(FP8X4),
+                rhs_scale=f_plane[PACK * kp :, c * CHUNK : (c + 1) * CHUNK],
+                start=(kp == 0),
+                stop=(kp == PASSES - 1),
+            )
+
+        def turn_q(u):
+            for h in range(2):
+                bank = next_bank()
+                q_banks[u, h] = bank
+                for i in range(TILES):
+                    words = q_raw[u][:, i, :].bitcast(F32)
+                    nc.tensor.transpose(bank[:, i * P : (i + 1) * P], words[:, h : 2 * P : 2], ident[:])
+
+        def tanh_q(u, slots):
+            g, c = units[u]
+            for t in slots:
+                tile = work.tile([P, CHUNK], F32, name="tanh%d" % t)
+                tanh_t[u, t] = tile
+                pairs = q_banks[u, t // 2][:].bitcast(BF16).rearrange("p (m e) -> p m e", e=2)
+                nc.scalar.activation(
+                    out=tile[:], in_=pairs[:, :, t % 2], func=ACT.Tanh, bias=zero_bias[:], scale=steep_col[:, g, t : t + 1]
+                )
+
+        def finish_y(u, t):
+            g, c = units[u]
+            if t == 0:
+                y_t[u] = work.tile([P, PACK, CHUNK], F32, name="y_t")
+            nc.vector.scalar_tensor_tensor(
+                out=y_t[u][:, t, :],
+                in0=tanh_t[u, t][:],
+                scalar=neg_fric_col[:, g, t : t + 1],
+                in1=tau[u, t][:],
+                op0=ALU.mult,
+                op1=ALU.add,
+            )
+
+        def turn_y(u, order):
+            for i in range(TILES):
+                y_banks[u, i] = next_bank()
+            for i, t in order:
+                nc.tensor.transpose(y_banks[u, i][:, t * P : (t + 1) * P], y_t[u][:, t, i * P : (i + 1) * P], ident[:])
+
+        def copy_y(u, i, engine):
+            if i == 0:
+                y_rows[u] = stage.tile([P, TILES, GROUP], F32, name="y_rows")
+            dst = y_rows[u][:, i, :].rearrange("m (p t) -> m p t", t=PACK)
+            src = y_banks[u, i][:].rearrange("m (t p) -> m p t", t=PACK)
+            if engine == "scalar":
+                nc.scalar.copy(out=dst, in_=src)
+            else:
+                nc.vector.tensor_copy(out=dst, in_=src)
+
+        def store_y(u, i0, i1):
+            g, c = units[u]
+            rows = out_0[c * CHUNK : (c + 1) * CHUNK, g * GROUP : (g + 1) * GROUP].rearrange("(i p) n -> p i n", p=P)
+            nc.sync.dma_start(out=rows[:, i0:i1, :], in_=y_rows[u][:, i0:i1, :])
+
+        def round_y(u):
+            y_bf[u] = work.tile([P, CHUNK, PACK], BF16, name="y_bf", align_bytes=64)
+            nc.vector.tensor_copy(
+                out=y_bf[u][:].rearrange("p (c i) t -> p c t i", i=4),
+                in_=y_t[u][:].rearrange("p t (c i) -> p c t i", i=4),
+            )
+
+        def quant_y(u):
+            g, c = units[u]
+            y_codes[u] = stage.tile([P, CHUNK], U32, name="y_codes", align_bytes=64)
+            nc.vector.quantize_mx(
+                out=y_codes[u][:].bitcast(FP8X4),
+                scales=y_planes[g][:, c * CHUNK : (c + 1) * CHUNK],
+                in_=y_bf[u][:].rearrange("p m t -> p (m t)"),
+            )
+
+        def store_codes(u):
+            g, c = units[u]
+            dst = out_1[g].rearrange("p m t -> p (m t)")[:, PACK * CHUNK * c : PACK * CHUNK * (c + 1)]
+            nc.sync.dma_start(out=dst.bitcast(I32), in_=y_codes[u][:].bitcast(I32))
+
+        def store_scales(g, m0, m1):
+            for q in range(4):
+                nc.sync.dma_start(
+                    out=out_2[g, 4 * q : 4 * q + 4, m0:m1].bitcast(I32),
+                    in_=y_planes[g][32 * q : 32 * q + 4, m0:m1].bitcast(I32),
+                )
+
+        tile_major = [(i, t) for i in range(TILES) for t in range(PACK)]
+        slot_major = [(i, t) for t in range(PACK) for i in range(TILES)]
+
+        nc.vector.memset(f_plane[:].bitcast(I32), 0)
+        make_identity(nc, ident[:])
+        nc.vector.memset(zero_in[:], 0.0)
+        nc.scalar.dma_start(out=steep_raw[:], in_=steep.rearrange("(g p t) -> p g t", p=P, t=PACK))
+        nc.scalar.dma_start(out=fric_raw[:], in_=friction.rearrange("(g p t) -> p g t", p=P, t=PACK))
+        nc.scalar.activation(out=zero_bias[:], in_=zero_in[:], func=ACT.Tanh)
+        for q in range(4):
+            nc.gpsimd.dma_start(
+                out=f_plane[32 * q : 32 * q + PACK * PASSES, :].bitcast(I32),
+                in_=f_scales[:, 4 * q : 4 * q + 4, :].bitcast(I32),
+            )
+        load_j(0, 0)
+        load_q(0)
+        load_f(0, [0])
+        load_j(1, 0)
+        load_f(0, [1])
+        load_j(2, 0)
+        load_f(0, [2])
+        load_q(1)
+        load_f(1, [0, 1, 2])
+        for c in range(2, CHUNKS):
+            load_j(c - 2, 1)
+            load_q(c)
+            load_f(c, [0, 1, 2])
+        load_j(2, 1)
+        load_q(CHUNKS)
+
+        for kp in range(PASSES):
+            group_j(kp, 0, 0)
+            group_j(kp, 0, 1)
+            if kp == 0:
+                nc.vector.tensor_copy(out=steep_col[:], in_=steep_raw[:])
+                nc.vector.tensor_scalar(
+                    out=neg_fric_col[:], in0=fric_raw[:], scalar1=-1.0, scalar2=None, op0=ALU.mult
+                )
+                turn_q(0)
+            quant_j(kp, 0, 0)
+            quant_j(kp, 0, 1)
+            tanh_q(0, [[0, 1], [2], [3]][kp])
+            for t in range(PACK):
+                mx_pass(0, t, kp)
+
+        for u in range(len(units)):
+            g, c = units[u]
+            prep = u - 1 if 1 <= u <= PASSES else None
+            for t in range(PACK):
+                if u > 0:
+                    for kp in range(PASSES):
+                        mx_pass(u, t, kp)
+                finish_y(u, t)
+                if prep is not None and t == 0:
+                    group_j(prep, 1, 0)
+                if prep is not None and t == 2:
+                    quant_j(prep, 1, 0)
+            if prep is not None:
+                group_j(prep, 1, 1)
+                quant_j(prep, 1, 1)
+            if u < last:
+                turn_q(u + 1)
+                tanh_q(u + 1, range(PACK))
+                turn_y(u, tile_major)
+                round_y(u)
+                quant_y(u)
+                for i in range(TILES):
+                    copy_y(u, i, "scalar")
+                store_codes(u)
+                store_y(u, 0, TILES)
+                if u + CHUNKS + 1 <= last:
+                    load_q(u + CHUNKS + 1)
+                if c == CHUNKS - 1:
+                    store_scales(g, 0, M)
+                if u == last - 1:
+                    store_scales(g, 0, M - CHUNK)
+            else:
+                turn_y(u, slot_major)
+                round_y(u)
+                quant_y(u)
+                for i in range(TILES - 1):
+                    copy_y(u, i, "scalar")
+                copy_y(u, TILES - 1, "vector")
+                store_y(u, 0, 1)
+                store_y(u, 1, 2)
+                store_codes(u)
+                store_scales(g, M - CHUNK, M)
+                store_y(u, 2, 3)
+                store_y(u, 3, 4)

@@ -48,7 +48,8 @@ def tile_joint_torque_friction_planes_g6_kernel(
             return psum.tile([P, CHUNK], F32, name="bank%d" % k)
 
         ident = keep.tile([P, P], F32, name="ident")
-        f_plane = keep.tile([P, M], U8, name="f_plane", align_bytes=64)
+        f_plane_a = keep.tile([P, PASSES, CHUNK], U8, name="f_plane_a", align_bytes=64)
+        f_plane_b = keep.tile([P, PASSES, M - CHUNK], U8, name="f_plane_b", align_bytes=64)
         zero_in = keep.tile([P, 1], F32, name="zero_in")
         zero_bias = keep.tile([P, 1], F32, name="zero_bias")
         steep_raw = keep.tile([P, GROUPS, PACK], BF16, name="steep_raw")
@@ -102,16 +103,16 @@ def tile_joint_torque_friction_planes_g6_kernel(
                 j_codes[kp, g, 2 * h + e] = codes[:, e * P : (e + 1) * P]
                 j_scales[kp, g, 2 * h + e] = scales[:, e * P : (e + 1) * P]
 
-        def mx_pass(u, t, kp):
+        def mx_pass(piece, t, kp):
+            u, m0, w = piece
             g, c = units[u]
-            if kp == 0:
-                tau[u, t] = next_bank()
+            plane = f_plane_a[:, kp, :] if c == 0 else f_plane_b[:, kp, (c - 1) * CHUNK : c * CHUNK]
             nc.tensor.matmul_mx(
-                out=tau[u, t][:],
+                out=tau[piece, t],
                 lhsT=j_codes[kp, g, t].bitcast(FP8X4),
                 lhsT_scale=j_scales[kp, g, t],
-                rhs=f_codes[kp, c].bitcast(FP8X4),
-                rhs_scale=f_plane[PACK * kp :, c * CHUNK : (c + 1) * CHUNK],
+                rhs=f_codes[kp, c][:, m0 : m0 + w].bitcast(FP8X4),
+                rhs_scale=plane[:, m0 : m0 + w],
                 start=(kp == 0),
                 stop=(kp == PASSES - 1),
             )
@@ -134,60 +135,83 @@ def tile_joint_torque_friction_planes_g6_kernel(
                     out=tile[:], in_=pairs[:, :, t % 2], func=ACT.Tanh, bias=zero_bias[:], scale=steep_col[:, g, t : t + 1]
                 )
 
-        def finish_y(u, t):
+        def open_tau(piece, slots):
+            bank = next_bank()
+            w = piece[2]
+            for e, t in enumerate(slots):
+                tau[piece, t] = bank[:, e * w : (e + 1) * w]
+
+        def multiply(piece, slots):
+            open_tau(piece, slots)
+            for t in slots:
+                for kp in range(PASSES):
+                    mx_pass(piece, t, kp)
+
+        def finish_y(piece, t):
+            u, m0, w = piece
             g, c = units[u]
             if t == 0:
-                y_t[u] = work.tile([P, PACK, CHUNK], F32, name="y_t")
+                y_t[piece] = work.tile([P, PACK, w], F32, name="y_t", bufs=3)
             nc.vector.scalar_tensor_tensor(
-                out=y_t[u][:, t, :],
-                in0=tanh_t[u, t][:],
+                out=y_t[piece][:, t, :],
+                in0=tanh_t[u, t][:, m0 : m0 + w],
                 scalar=neg_fric_col[:, g, t : t + 1],
-                in1=tau[u, t][:],
+                in1=tau[piece, t],
                 op0=ALU.mult,
                 op1=ALU.add,
             )
 
-        def turn_y(u, order):
-            for i in range(TILES):
-                y_banks[u, i] = next_bank()
-            for i, t in order:
-                nc.tensor.transpose(y_banks[u, i][:, t * P : (t + 1) * P], y_t[u][:, t, i * P : (i + 1) * P], ident[:])
-
-        def copy_y(u, i, engine):
-            if i == 0:
-                y_rows[u] = stage.tile([P, TILES, GROUP], F32, name="y_rows")
-            dst = y_rows[u][:, i, :].rearrange("m (p t) -> m p t", t=PACK)
-            src = y_banks[u, i][:].rearrange("m (t p) -> m p t", t=PACK)
-            if engine == "scalar":
-                nc.scalar.copy(out=dst, in_=src)
+        def turn_y(piece, slot_major):
+            tiles = piece[2] // P
+            for i in range(tiles):
+                y_banks[piece, i] = next_bank()
+            if slot_major:
+                order = [(i, t) for t in range(PACK) for i in range(tiles)]
             else:
-                nc.vector.tensor_copy(out=dst, in_=src)
+                order = [(i, t) for i in range(tiles) for t in range(PACK)]
+            for i, t in order:
+                nc.tensor.transpose(
+                    y_banks[piece, i][:, t * P : (t + 1) * P], y_t[piece][:, t, i * P : (i + 1) * P], ident[:]
+                )
 
-        def store_y(u, i0, i1):
+        def copy_y(piece, i):
+            if i == 0:
+                y_rows[piece] = stage.tile([P, piece[2] // P, GROUP], F32, name="y_rows", bufs=5)
+            dst = y_rows[piece][:, i, :].rearrange("m (p t) -> m p t", t=PACK)
+            src = y_banks[piece, i][:].rearrange("m (t p) -> m p t", t=PACK)
+            nc.scalar.copy(out=dst, in_=src)
+
+        def store_y(piece, i0, i1, engine):
+            u, m0, w = piece
             g, c = units[u]
-            rows = out_0[c * CHUNK : (c + 1) * CHUNK, g * GROUP : (g + 1) * GROUP].rearrange("(i p) n -> p i n", p=P)
-            nc.sync.dma_start(out=rows[:, i0:i1, :], in_=y_rows[u][:, i0:i1, :])
+            r0 = c * CHUNK + m0
+            rows = out_0[r0 : r0 + w, g * GROUP : (g + 1) * GROUP].rearrange("(i p) n -> p i n", p=P)
+            engine.dma_start(out=rows[:, i0:i1, :], in_=y_rows[piece][:, i0:i1, :])
 
-        def round_y(u):
-            y_bf[u] = work.tile([P, CHUNK, PACK], BF16, name="y_bf", align_bytes=64)
+        def round_y(piece):
+            y_bf[piece] = work.tile([P, piece[2], PACK], BF16, name="y_bf", align_bytes=64)
             nc.vector.tensor_copy(
-                out=y_bf[u][:].rearrange("p (c i) t -> p c t i", i=4),
-                in_=y_t[u][:].rearrange("p t (c i) -> p c t i", i=4),
+                out=y_bf[piece][:].rearrange("p (c i) t -> p c t i", i=4),
+                in_=y_t[piece][:].rearrange("p t (c i) -> p c t i", i=4),
             )
 
-        def quant_y(u):
+        def quant_y(piece):
+            u, m0, w = piece
             g, c = units[u]
-            y_codes[u] = stage.tile([P, CHUNK], U32, name="y_codes", align_bytes=64)
+            r0 = c * CHUNK + m0
+            y_codes[piece] = stage.tile([P, w], U32, name="y_codes", align_bytes=64)
             nc.vector.quantize_mx(
-                out=y_codes[u][:].bitcast(FP8X4),
-                scales=y_planes[g][:, c * CHUNK : (c + 1) * CHUNK],
-                in_=y_bf[u][:].rearrange("p m t -> p (m t)"),
+                out=y_codes[piece][:].bitcast(FP8X4),
+                scales=y_planes[g][:, r0 : r0 + w],
+                in_=y_bf[piece][:].rearrange("p m t -> p (m t)"),
             )
 
-        def store_codes(u):
+        def store_codes(piece):
+            u, m0, w = piece
             g, c = units[u]
-            dst = out_1[g].rearrange("p m t -> p (m t)")[:, PACK * CHUNK * c : PACK * CHUNK * (c + 1)]
-            nc.sync.dma_start(out=dst.bitcast(I32), in_=y_codes[u][:].bitcast(I32))
+            r0 = c * CHUNK + m0
+            dst = out_1[g].rearrange("p m t -> p (m t)")[:, PACK * r0 : PACK * (r0 + w)]
+            nc.sync.dma_start(out=dst.bitcast(I32), in_=y_codes[piece][:].bitcast(I32))
 
         def store_scales(g, m0, m1):
             for q in range(4):
@@ -196,28 +220,30 @@ def tile_joint_torque_friction_planes_g6_kernel(
                     in_=y_planes[g][32 * q : 32 * q + 4, m0:m1].bitcast(I32),
                 )
 
-        tile_major = [(i, t) for i in range(TILES) for t in range(PACK)]
-        slot_major = [(i, t) for t in range(PACK) for i in range(TILES)]
+        def load_f_scales(engine, plane, m0, m1):
+            for r in range(4):
+                engine.dma_start(
+                    out=plane[r:P:32, :, :].bitcast(I32),
+                    in_=f_scales[:, r:16:4, m0:m1].rearrange("g q m -> q g m").bitcast(I32),
+                )
 
-        nc.vector.memset(f_plane[:].bitcast(I32), 0)
-        make_identity(nc, ident[:])
+        nc.vector.memset(f_plane_a[:].bitcast(I32), 0)
         nc.vector.memset(zero_in[:], 0.0)
-        nc.scalar.dma_start(out=steep_raw[:], in_=steep.rearrange("(g p t) -> p g t", p=P, t=PACK))
-        nc.scalar.dma_start(out=fric_raw[:], in_=friction.rearrange("(g p t) -> p g t", p=P, t=PACK))
-        nc.scalar.activation(out=zero_bias[:], in_=zero_in[:], func=ACT.Tanh)
-        for q in range(4):
-            nc.gpsimd.dma_start(
-                out=f_plane[32 * q : 32 * q + PACK * PASSES, :].bitcast(I32),
-                in_=f_scales[:, 4 * q : 4 * q + 4, :].bitcast(I32),
-            )
+        nc.vector.memset(f_plane_b[:].bitcast(I32), 0)
+        make_identity(nc, ident[:])
         load_j(0, 0)
         load_q(0)
+        nc.scalar.activation(out=zero_bias[:], in_=zero_in[:], func=ACT.Tanh)
+        nc.sync.dma_start(out=steep_raw[:], in_=steep.rearrange("(g p t) -> p g t", p=P, t=PACK))
         load_f(0, [0])
+        load_f_scales(nc.sync, f_plane_a, 0, CHUNK)
         load_j(1, 0)
+        nc.sync.dma_start(out=fric_raw[:], in_=friction.rearrange("(g p t) -> p g t", p=P, t=PACK))
         load_f(0, [1])
         load_j(2, 0)
         load_f(0, [2])
         load_q(1)
+        load_f_scales(nc.sync, f_plane_b, CHUNK, M)
         load_f(1, [0, 1, 2])
         for c in range(2, CHUNKS):
             load_j(c - 2, 1)
@@ -231,24 +257,27 @@ def tile_joint_torque_friction_planes_g6_kernel(
             group_j(kp, 0, 1)
             if kp == 0:
                 nc.vector.tensor_copy(out=steep_col[:], in_=steep_raw[:])
+                turn_q(0)
+            if kp == 1:
                 nc.vector.tensor_scalar(
                     out=neg_fric_col[:], in0=fric_raw[:], scalar1=-1.0, scalar2=None, op0=ALU.mult
                 )
-                turn_q(0)
             quant_j(kp, 0, 0)
             quant_j(kp, 0, 1)
             tanh_q(0, [[0, 1], [2], [3]][kp])
             for t in range(PACK):
-                mx_pass(0, t, kp)
+                if kp == 0:
+                    open_tau((0, 0, CHUNK), [t])
+                mx_pass((0, 0, CHUNK), t, kp)
 
-        for u in range(len(units)):
+        for u in range(last):
             g, c = units[u]
+            piece = (u, 0, CHUNK)
             prep = u - 1 if 1 <= u <= PASSES else None
             for t in range(PACK):
                 if u > 0:
-                    for kp in range(PASSES):
-                        mx_pass(u, t, kp)
-                finish_y(u, t)
+                    multiply(piece, [t])
+                finish_y(piece, t)
                 if prep is not None and t == 0:
                     group_j(prep, 1, 0)
                 if prep is not None and t == 2:
@@ -256,32 +285,52 @@ def tile_joint_torque_friction_planes_g6_kernel(
             if prep is not None:
                 group_j(prep, 1, 1)
                 quant_j(prep, 1, 1)
-            if u < last:
-                turn_q(u + 1)
-                tanh_q(u + 1, range(PACK))
-                turn_y(u, tile_major)
-                round_y(u)
-                quant_y(u)
-                for i in range(TILES):
-                    copy_y(u, i, "scalar")
-                store_codes(u)
-                store_y(u, 0, TILES)
-                if u + CHUNKS + 1 <= last:
-                    load_q(u + CHUNKS + 1)
-                if c == CHUNKS - 1:
-                    store_scales(g, 0, M)
-                if u == last - 1:
-                    store_scales(g, 0, M - CHUNK)
-            else:
-                turn_y(u, slot_major)
-                round_y(u)
-                quant_y(u)
-                for i in range(TILES - 1):
-                    copy_y(u, i, "scalar")
-                copy_y(u, TILES - 1, "vector")
-                store_y(u, 0, 1)
-                store_y(u, 1, 2)
-                store_codes(u)
-                store_scales(g, M - CHUNK, M)
-                store_y(u, 2, 3)
-                store_y(u, 3, 4)
+            turn_q(u + 1)
+            tanh_q(u + 1, range(PACK))
+            turn_y(piece, False)
+            round_y(piece)
+            quant_y(piece)
+            for i in range(TILES):
+                copy_y(piece, i)
+            store_codes(piece)
+            if c == CHUNKS - 1:
+                store_scales(g, 0, M)
+            if u == last - 1:
+                store_scales(g, 0, M - CHUNK)
+            store_y(piece, 0, 2, nc.sync)
+            store_y(piece, 2, TILES, nc.sync)
+            if u + CHUNKS + 1 <= last:
+                load_q(u + CHUNKS + 1)
+
+        pa, pb, pc = (last, 0, 2 * P), (last, 2 * P, P), (last, 3 * P, P)
+        for t in range(PACK):
+            multiply(pa, [t])
+            finish_y(pa, t)
+        round_y(pa)
+        for h in range(2):
+            multiply(pb, [2 * h, 2 * h + 1])
+            finish_y(pb, 2 * h)
+            finish_y(pb, 2 * h + 1)
+        quant_y(pa)
+        turn_y(pa, False)
+        turn_y(pb, False)
+        round_y(pb)
+        store_codes(pa)
+        for i in range(2):
+            copy_y(pa, i)
+            store_y(pa, i, i + 1, nc.sync)
+        copy_y(pb, 0)
+        for t in range(PACK):
+            multiply(pc, [t])
+            finish_y(pc, t)
+            if t == 0:
+                quant_y(pb)
+        store_codes(pb)
+        store_y(pb, 0, 1, nc.sync)
+        turn_y(pc, True)
+        round_y(pc)
+        quant_y(pc)
+        copy_y(pc, 0)
+        store_codes(pc)
+        store_scales(GROUPS - 1, M - CHUNK, M)
+        store_y(pc, 0, 1, nc.scalar)

@@ -56,11 +56,12 @@ def tile_joint_torque_friction_planes_g6_kernel(
         fric_raw = keep.tile([P, GROUPS, PACK], BF16, name="fric_raw")
         steep_col = keep.tile([P, GROUPS, PACK], F32, name="steep_col")
         neg_fric_col = keep.tile([P, GROUPS, PACK], F32, name="neg_fric_col")
-        y_planes = [keep.tile([P, M], U8, name="y_plane%d" % g, align_bytes=64) for g in range(GROUPS)]
+        y_planes = [keep.tile([P, CHUNK], U8, name="y_plane%d" % g, align_bytes=64) for g in range(GROUPS)]
 
         j_raw, j_grouped, j_codes, j_scales = {}, {}, {}, {}
         f_codes, q_raw, q_banks, tanh_t, tau, y_t, y_banks, y_rows, y_bf, y_codes = ({} for i in range(10))
 
+        q_split = {}
         f_view = f_words.rearrange("g p m t -> p g (m t)")
 
         def load_j(kp, g):
@@ -103,6 +104,37 @@ def tile_joint_torque_friction_planes_g6_kernel(
                 j_codes[kp, g, 2 * h + e] = codes[:, e * P : (e + 1) * P]
                 j_scales[kp, g, 2 * h + e] = scales[:, e * P : (e + 1) * P]
 
+        def group_late_vector(kp):
+            tile = stage.tile([P, 1, P, PACK], BF16, name="j_grouped", align_bytes=64)
+            j_grouped[kp, 1, 0] = tile
+            src = j_raw[kp, 1][:].rearrange("p j (m t) -> p t m j", t=PACK)
+            nc.vector.tensor_copy(out=tile[:, 0, :, :], in_=src[:, 0, :, :])
+
+        def group_late_gpsimd(kp):
+            tile = work.tile([P, PACK - 1, P, PACK], BF16, name="y_bf", bufs=1, align_bytes=64)
+            j_grouped[kp, 1, 1] = tile
+            src = j_raw[kp, 1][:].rearrange("p j (m t) -> p t m j", t=PACK)
+            for t in range(1, PACK):
+                nc.gpsimd.tensor_scalar(
+                    out=tile[:, t - 1, :, :], in0=src[:, t, :, :], scalar1=1.0, scalar2=0.0, op0=ALU.mult, op1=ALU.add
+                )
+
+        def quant_late(kp, src, t0, t1):
+            w = (t1 - t0) * P
+            codes = keep.tile([P, w], U32, name="j_codes%d_1_%d" % (kp, t0), align_bytes=64)
+            scales = keep.tile([P, w], U8, name="j_scales%d_1_%d" % (kp, t0), align_bytes=64)
+            nc.vector.quantize_mx(
+                out=codes[:].bitcast(FP8X4), scales=scales[:], in_=src.rearrange("p t m j -> p (t m j)")
+            )
+            for t in range(t0, t1):
+                j_codes[kp, 1, t] = codes[:, (t - t0) * P : (t - t0 + 1) * P]
+                j_scales[kp, 1, t] = scales[:, (t - t0) * P : (t - t0 + 1) * P]
+
+        def split_q(u):
+            q_split[u] = work.tile([P, TILES, 2, P], F32, name="q_split")
+            words = q_raw[u][:].bitcast(F32).rearrange("p i (w h) -> p i h w", h=2)
+            nc.vector.tensor_copy(out=q_split[u][:], in_=words)
+
         def mx_pass(piece, t, kp):
             u, m0, w = piece
             g, c = units[u]
@@ -122,8 +154,11 @@ def tile_joint_torque_friction_planes_g6_kernel(
                 bank = next_bank()
                 q_banks[u, h] = bank
                 for i in range(TILES):
-                    words = q_raw[u][:, i, :].bitcast(F32)
-                    nc.tensor.transpose(bank[:, i * P : (i + 1) * P], words[:, h : 2 * P : 2], ident[:])
+                    if u in q_split:
+                        words = q_split[u][:, i, h, :]
+                    else:
+                        words = q_raw[u][:, i, :].bitcast(F32)[:, h : 2 * P : 2]
+                    nc.tensor.transpose(bank[:, i * P : (i + 1) * P], words, ident[:])
 
         def tanh_q(u, slots):
             g, c = units[u]
@@ -189,7 +224,7 @@ def tile_joint_torque_friction_planes_g6_kernel(
             engine.dma_start(out=rows[:, i0:i1, :], in_=y_rows[piece][:, i0:i1, :])
 
         def round_y(piece):
-            y_bf[piece] = work.tile([P, piece[2], PACK], BF16, name="y_bf", align_bytes=64)
+            y_bf[piece] = work.tile([P, piece[2], PACK], BF16, name="y_bf", bufs=1, align_bytes=64)
             nc.vector.tensor_copy(
                 out=y_bf[piece][:].rearrange("p (c i) t -> p c t i", i=4),
                 in_=y_t[piece][:].rearrange("p t (c i) -> p c t i", i=4),
@@ -198,11 +233,10 @@ def tile_joint_torque_friction_planes_g6_kernel(
         def quant_y(piece):
             u, m0, w = piece
             g, c = units[u]
-            r0 = c * CHUNK + m0
             y_codes[piece] = stage.tile([P, w], U32, name="y_codes", align_bytes=64)
             nc.vector.quantize_mx(
                 out=y_codes[piece][:].bitcast(FP8X4),
-                scales=y_planes[g][:, r0 : r0 + w],
+                scales=y_planes[g][4 * c :, m0 : m0 + w],
                 in_=y_bf[piece][:].rearrange("p m t -> p (m t)"),
             )
 
@@ -213,11 +247,11 @@ def tile_joint_torque_friction_planes_g6_kernel(
             dst = out_1[g].rearrange("p m t -> p (m t)")[:, PACK * r0 : PACK * (r0 + w)]
             nc.sync.dma_start(out=dst.bitcast(I32), in_=y_codes[piece][:].bitcast(I32))
 
-        def store_scales(g, m0, m1):
+        def store_scales(g):
             for q in range(4):
                 nc.sync.dma_start(
-                    out=out_2[g, 4 * q : 4 * q + 4, m0:m1].bitcast(I32),
-                    in_=y_planes[g][32 * q : 32 * q + 4, m0:m1].bitcast(I32),
+                    out=out_2[g, 4 * q : 4 * q + 4, :].rearrange("r (c m) -> c r m", c=CHUNKS).bitcast(I32),
+                    in_=y_planes[g][32 * q : 32 * q + 4 * CHUNKS, :].bitcast(I32),
                 )
 
         def load_f_scales(engine, plane, m0, m1):
@@ -239,8 +273,8 @@ def tile_joint_torque_friction_planes_g6_kernel(
         load_f_scales(nc.sync, f_plane_a, 0, CHUNK)
         load_j(1, 0)
         nc.sync.dma_start(out=fric_raw[:], in_=friction.rearrange("(g p t) -> p g t", p=P, t=PACK))
-        load_f(0, [1])
         load_j(2, 0)
+        load_f(0, [1])
         load_f(0, [2])
         load_q(1)
         load_f_scales(nc.sync, f_plane_b, CHUNK, M)
@@ -278,29 +312,33 @@ def tile_joint_torque_friction_planes_g6_kernel(
                 if u > 0:
                     multiply(piece, [t])
                 finish_y(piece, t)
-                if prep is not None and t == 0:
-                    group_j(prep, 1, 0)
-                if prep is not None and t == 2:
-                    quant_j(prep, 1, 0)
+                if prep == 0 and t == 0:
+                    group_late_vector(prep)
+                if prep is not None and t == 1:
+                    quant_late(prep, j_grouped[prep, 1, 0][:], 0, 1)
             if prep is not None:
-                group_j(prep, 1, 1)
-                quant_j(prep, 1, 1)
+                quant_late(prep, j_grouped[prep, 1, 1][:, 0:1, :, :], 1, 2)
+                quant_late(prep, j_grouped[prep, 1, 1][:, 1:3, :, :], 2, 4)
             turn_q(u + 1)
             tanh_q(u + 1, range(PACK))
             turn_y(piece, False)
             round_y(piece)
+            if 1 <= u < PASSES:
+                group_late_vector(u)
+            if PASSES <= u < last - 1:
+                split_q(u + 2)
             quant_y(piece)
+            if u < PASSES:
+                group_late_gpsimd(u)
             for i in range(TILES):
                 copy_y(piece, i)
-            store_codes(piece)
-            if c == CHUNKS - 1:
-                store_scales(g, 0, M)
-            if u == last - 1:
-                store_scales(g, 0, M - CHUNK)
-            store_y(piece, 0, 2, nc.sync)
-            store_y(piece, 2, TILES, nc.sync)
             if u + CHUNKS + 1 <= last:
                 load_q(u + CHUNKS + 1)
+            store_codes(piece)
+            if c == CHUNKS - 1:
+                store_scales(g)
+            store_y(piece, 0, 2, nc.sync)
+            store_y(piece, 2, TILES, nc.sync)
 
         pa, pb, pc = (last, 0, 2 * P), (last, 2 * P, P), (last, 3 * P, P)
         for t in range(PACK):
@@ -332,5 +370,5 @@ def tile_joint_torque_friction_planes_g6_kernel(
         quant_y(pc)
         copy_y(pc, 0)
         store_codes(pc)
-        store_scales(GROUPS - 1, M - CHUNK, M)
+        store_scales(GROUPS - 1)
         store_y(pc, 0, 1, nc.scalar)

@@ -49,7 +49,8 @@ def tile_joint_torque_friction_planes_g6_kernel(
 
         ident = keep.tile([P, P], F32, name="ident")
         f_plane_a = keep.tile([P, PASSES, CHUNK], U8, name="f_plane_a", align_bytes=64)
-        f_plane_b = keep.tile([P, PASSES, M - CHUNK], U8, name="f_plane_b", align_bytes=64)
+        f_plane_b = keep.tile([P, PASSES, CHUNK], U8, name="f_plane_b", align_bytes=64)
+        f_plane_c = keep.tile([P, PASSES, 2 * CHUNK], U8, name="f_plane_c", align_bytes=64)
         zero_in = keep.tile([P, 1], F32, name="zero_in")
         zero_bias = keep.tile([P, 1], F32, name="zero_bias")
         steep_raw = keep.tile([P, GROUPS, PACK], BF16, name="steep_raw")
@@ -104,32 +105,6 @@ def tile_joint_torque_friction_planes_g6_kernel(
                 j_codes[kp, g, 2 * h + e] = codes[:, e * P : (e + 1) * P]
                 j_scales[kp, g, 2 * h + e] = scales[:, e * P : (e + 1) * P]
 
-        def group_late_vector(kp):
-            tile = stage.tile([P, 1, P, PACK], BF16, name="j_grouped", align_bytes=64)
-            j_grouped[kp, 1, 0] = tile
-            src = j_raw[kp, 1][:].rearrange("p j (m t) -> p t m j", t=PACK)
-            nc.vector.tensor_copy(out=tile[:, 0, :, :], in_=src[:, 0, :, :])
-
-        def group_late_gpsimd(kp):
-            tile = work.tile([P, PACK - 1, P, PACK], BF16, name="y_bf", bufs=1, align_bytes=64)
-            j_grouped[kp, 1, 1] = tile
-            src = j_raw[kp, 1][:].rearrange("p j (m t) -> p t m j", t=PACK)
-            for t in range(1, PACK):
-                nc.gpsimd.tensor_scalar(
-                    out=tile[:, t - 1, :, :], in0=src[:, t, :, :], scalar1=1.0, scalar2=0.0, op0=ALU.mult, op1=ALU.add
-                )
-
-        def quant_late(kp, src, t0, t1):
-            w = (t1 - t0) * P
-            codes = keep.tile([P, w], U32, name="j_codes%d_1_%d" % (kp, t0), align_bytes=64)
-            scales = keep.tile([P, w], U8, name="j_scales%d_1_%d" % (kp, t0), align_bytes=64)
-            nc.vector.quantize_mx(
-                out=codes[:].bitcast(FP8X4), scales=scales[:], in_=src.rearrange("p t m j -> p (t m j)")
-            )
-            for t in range(t0, t1):
-                j_codes[kp, 1, t] = codes[:, (t - t0) * P : (t - t0 + 1) * P]
-                j_scales[kp, 1, t] = scales[:, (t - t0) * P : (t - t0 + 1) * P]
-
         def split_q(u):
             q_split[u] = work.tile([P, TILES, 2, P], F32, name="q_split")
             words = q_raw[u][:].bitcast(F32).rearrange("p i (w h) -> p i h w", h=2)
@@ -138,7 +113,7 @@ def tile_joint_torque_friction_planes_g6_kernel(
         def mx_pass(piece, t, kp):
             u, m0, w = piece
             g, c = units[u]
-            plane = f_plane_a[:, kp, :] if c == 0 else f_plane_b[:, kp, (c - 1) * CHUNK : c * CHUNK]
+            plane = [f_plane_a[:, kp, :], f_plane_b[:, kp, :], f_plane_c[:, kp, :CHUNK], f_plane_c[:, kp, CHUNK:]][c]
             nc.tensor.matmul_mx(
                 out=tau[piece, t],
                 lhsT=j_codes[kp, g, t].bitcast(FP8X4),
@@ -224,7 +199,7 @@ def tile_joint_torque_friction_planes_g6_kernel(
             engine.dma_start(out=rows[:, i0:i1, :], in_=y_rows[piece][:, i0:i1, :])
 
         def round_y(piece):
-            y_bf[piece] = work.tile([P, piece[2], PACK], BF16, name="y_bf", bufs=1, align_bytes=64)
+            y_bf[piece] = work.tile([P, piece[2], PACK], BF16, name="y_bf", align_bytes=64)
             nc.vector.tensor_copy(
                 out=y_bf[piece][:].rearrange("p (c i) t -> p c t i", i=4),
                 in_=y_t[piece][:].rearrange("p t (c i) -> p c t i", i=4),
@@ -264,6 +239,7 @@ def tile_joint_torque_friction_planes_g6_kernel(
         nc.vector.memset(f_plane_a[:].bitcast(I32), 0)
         nc.vector.memset(zero_in[:], 0.0)
         nc.vector.memset(f_plane_b[:].bitcast(I32), 0)
+        nc.vector.memset(f_plane_c[:].bitcast(I32), 0)
         make_identity(nc, ident[:])
         load_j(0, 0)
         load_q(0)
@@ -277,11 +253,13 @@ def tile_joint_torque_friction_planes_g6_kernel(
         load_f(0, [1])
         load_f(0, [2])
         load_q(1)
-        load_f_scales(nc.sync, f_plane_b, CHUNK, M)
+        load_f_scales(nc.sync, f_plane_b, CHUNK, 2 * CHUNK)
         load_f(1, [0, 1, 2])
         for c in range(2, CHUNKS):
             load_j(c - 2, 1)
             load_q(c)
+            if c == 2:
+                load_f_scales(nc.sync, f_plane_c, 2 * CHUNK, M)
             load_f(c, [0, 1, 2])
         load_j(2, 1)
         load_q(CHUNKS)
@@ -304,32 +282,9 @@ def tile_joint_torque_friction_planes_g6_kernel(
                     open_tau((0, 0, CHUNK), [t])
                 mx_pass((0, 0, CHUNK), t, kp)
 
-        for u in range(last):
+        def drain_rows(piece):
+            u = piece[0]
             g, c = units[u]
-            piece = (u, 0, CHUNK)
-            prep = u - 1 if 1 <= u <= PASSES else None
-            for t in range(PACK):
-                if u > 0:
-                    multiply(piece, [t])
-                finish_y(piece, t)
-                if prep == 0 and t == 0:
-                    group_late_vector(prep)
-                if prep is not None and t == 1:
-                    quant_late(prep, j_grouped[prep, 1, 0][:], 0, 1)
-            if prep is not None:
-                quant_late(prep, j_grouped[prep, 1, 1][:, 0:1, :, :], 1, 2)
-                quant_late(prep, j_grouped[prep, 1, 1][:, 1:3, :, :], 2, 4)
-            turn_q(u + 1)
-            tanh_q(u + 1, range(PACK))
-            turn_y(piece, False)
-            round_y(piece)
-            if 1 <= u < PASSES:
-                group_late_vector(u)
-            if PASSES <= u < last - 1:
-                split_q(u + 2)
-            quant_y(piece)
-            if u < PASSES:
-                group_late_gpsimd(u)
             for i in range(TILES):
                 copy_y(piece, i)
             if u + CHUNKS + 1 <= last:
@@ -340,28 +295,75 @@ def tile_joint_torque_friction_planes_g6_kernel(
             store_y(piece, 0, 2, nc.sync)
             store_y(piece, 2, TILES, nc.sync)
 
-        pa, pb, pc = (last, 0, 2 * P), (last, 2 * P, P), (last, 3 * P, P)
+        first = (0, 0, CHUNK)
         for t in range(PACK):
+            finish_y(first, t)
+        turn_q(1)
+        tanh_q(1, range(PACK))
+        turn_y(first, False)
+
+        for u in range(1, last):
+            piece, before = (u, 0, CHUNK), (u - 1, 0, CHUNK)
+            prep = u - 1 if u <= PASSES else None
+            round_y(before)
+            multiply(piece, [0])
+            finish_y(piece, 0)
+            quant_y(before)
+            multiply(piece, [1])
+            finish_y(piece, 1)
+            if u > 1:
+                if prep is not None:
+                    group_j(prep, 1, 1)
+                turn_y(before, False)
+            drain_rows(before)
+            if prep is None:
+                split_q(u + 1)
+            else:
+                if u == 1:
+                    group_j(prep, 1, 1)
+                group_j(prep, 1, 0)
+            multiply(piece, [2])
+            finish_y(piece, 2)
+            if prep is not None:
+                quant_j(prep, 1, 0)
+            multiply(piece, [3])
+            finish_y(piece, 3)
+            if prep is not None:
+                quant_j(prep, 1, 1)
+            turn_q(u + 1)
+            tanh_q(u + 1, range(PACK))
+
+        before = (last - 1, 0, CHUNK)
+        pa, pb, pc = (last, 0, 2 * P), (last, 2 * P, P), (last, 3 * P, P)
+        round_y(before)
+        for t in range(2):
             multiply(pa, [t])
             finish_y(pa, t)
-        round_y(pa)
+        quant_y(before)
+        turn_y(before, False)
+        drain_rows(before)
+        for t in range(2, PACK):
+            multiply(pa, [t])
+            finish_y(pa, t)
         for h in range(2):
             multiply(pb, [2 * h, 2 * h + 1])
             finish_y(pb, 2 * h)
             finish_y(pb, 2 * h + 1)
-        quant_y(pa)
         turn_y(pa, False)
         turn_y(pb, False)
+        round_y(pa)
         round_y(pb)
-        store_codes(pa)
+        quant_y(pa)
         for i in range(2):
             copy_y(pa, i)
-            store_y(pa, i, i + 1, nc.sync)
         copy_y(pb, 0)
+        store_y(pa, 0, 1, nc.sync)
+        store_codes(pa)
+        store_y(pa, 1, 2, nc.sync)
         for t in range(PACK):
             multiply(pc, [t])
             finish_y(pc, t)
-            if t == 0:
+            if t == 1:
                 quant_y(pb)
         store_codes(pb)
         store_y(pb, 0, 1, nc.sync)

from contextlib import ExitStack

import concourse.mybir as mybir
from concourse.masks import make_identity

M, K, N = 2048, 1536, 1024
FLOPS = 2 * M * K * N

F32 = mybir.dt.float32
BF16 = mybir.dt.bfloat16
I32 = mybir.dt.int32
U32 = mybir.dt.uint32
U8 = mybir.dt.uint8
FP8X4 = mybir.dt.float8_e4m3fn_x4
ALU = mybir.AluOpType
ACT = mybir.ActivationFunctionType

P = 128
PACK = 4
GROUP = P * PACK
PASSES = K // GROUP
GROUPS = N // GROUP
CHUNK = 512
CHUNKS = M // CHUNK
TILES = CHUNK // P
BANKS = 8


def tile_joint_torque_friction_planes_g6_kernel(
    tc, f_words, f_scales, jac, qd, friction, steep, out_0, out_1, out_2
):
    nc = tc.nc
    units = [(g, c) for g in range(GROUPS) for c in range(CHUNKS)]
    last = len(units) - 1

    with ExitStack() as ctx:
        keep = ctx.enter_context(tc.tile_pool(name="keep", bufs=1))
        work = ctx.enter_context(tc.tile_pool(name="work", bufs=2))
        stage = ctx.enter_context(tc.tile_pool(name="stage", bufs=4))
        psum = ctx.enter_context(tc.psum_pool(name="psum", bufs=1))
        ctx.enter_context(tc.manual_schedule())

        ring = []

        def next_bank():
            k = len(ring) % BANKS
            ring.append(k)
            return psum.tile([P, CHUNK], F32, name="bank%d" % k)

        ident = keep.tile([P, P], F32, name="ident")
        f_plane_a = keep.tile([P, PASSES, CHUNK], U8, name="f_plane_a", align_bytes=64)
        f_plane_b = keep.tile([P, PASSES, CHUNK], U8, name="f_plane_b", align_bytes=64)
        f_plane_c = keep.tile([P, PASSES, 2 * CHUNK], U8, name="f_plane_c", align_bytes=64)
        zero_in = keep.tile([P, 1], F32, name="zero_in")
        zero_bias = keep.tile([P, 1], F32, name="zero_bias")
        steep_raw = keep.tile([P, GROUPS, PACK], BF16, name="steep_raw")
        fric_raw = keep.tile([P, GROUPS, PACK], BF16, name="fric_raw")
        steep_col = keep.tile([P, GROUPS, PACK], F32, name="steep_col")
        neg_fric_col = keep.tile([P, GROUPS, PACK], F32, name="neg_fric_col")
        y_planes = [keep.tile([P, CHUNK], U8, name="y_plane%d" % g, align_bytes=64) for g in range(GROUPS)]

        j_raw, j_grouped, j_codes, j_scales = {}, {}, {}, {}
        f_codes, q_raw, q_banks, tanh_t, tau, y_t, y_banks, y_rows, y_bf, y_codes = ({} for i in range(10))

        q_split = {}
        f_view = f_words.rearrange("g p m t -> p g (m t)")

        def load_j(kp, g):
            j_raw[kp, g] = keep.tile([P, PACK, GROUP], BF16, name="j_raw%d_%d" % (kp, g))
            rows = jac[kp * GROUP : (kp + 1) * GROUP, g * GROUP : (g + 1) * GROUP]
            nc.sync.dma_start(out=j_raw[kp, g][:], in_=rows.rearrange("(p j) n -> p j n", j=PACK))

        def load_f(c, kps):
            tile = keep.tile([P, len(kps), CHUNK], U32, name="f_codes%d_%d" % (c, kps[0]), align_bytes=64)
            src = f_view[:, kps[0] : kps[-1] + 1, PACK * CHUNK * c : PACK * CHUNK * (c + 1)]
            nc.sync.dma_start(out=tile[:].bitcast(I32), in_=src.bitcast(I32))
            for i, kp in enumerate(kps):
                f_codes[kp, c] = tile[:, i, :]

        def load_q(u):
            g, c = units[u]
            q_raw[u] = keep.tile([P, TILES, GROUP], BF16, name="q_raw%d" % u)
            rows = qd[c * CHUNK : (c + 1) * CHUNK, g * GROUP : (g + 1) * GROUP]
            nc.sync.dma_start(out=q_raw[u][:], in_=rows.rearrange("(i p) n -> p i n", p=P))

        def group_j(kp, g, h):
            tile = stage.tile([P, 2, P, PACK], BF16, name="j_grouped", align_bytes=64)
            j_grouped[kp, g, h] = tile
            src = j_raw[kp, g][:].rearrange("p j (m t) -> p m j t", t=PACK)[:, :, :, 2 * h : 2 * h + 2]
            dst = tile[:].rearrange("p t m j -> p m j t")
            if h == 0:
                nc.vector.tensor_copy(out=dst, in_=src)
            else:
                nc.scalar.copy(out=dst, in_=src)

        def quant_j(kp, g, h):
            codes = keep.tile([P, 2 * P], U32, name="j_codes%d_%d_%d" % (kp, g, h), align_bytes=64)
            scales = keep.tile([P, 2 * P], U8, name="j_scales%d_%d_%d" % (kp, g, h), align_bytes=64)
            nc.vector.quantize_mx(
                out=codes[:].bitcast(FP8X4),
                scales=scales[:],
                in_=j_grouped[kp, g, h][:].rearrange("p t m j -> p (t m j)"),
            )
            for e in range(2):
                j_codes[kp, g, 2 * h + e] = codes[:, e * P : (e + 1) * P]
                j_scales[kp, g, 2 * h + e] = scales[:, e * P : (e + 1) * P]

        def split_q(u):
            q_split[u] = work.tile([P, TILES, 2, P], F32, name="q_split")
            words = q_raw[u][:].bitcast(F32).rearrange("p i (w h) -> p i h w", h=2)
            nc.vector.tensor_copy(out=q_split[u][:], in_=words)

        def mx_pass(piece, t, kp):
            u, m0, w = piece
            g, c = units[u]
            plane = [f_plane_a[:, kp, :], f_plane_b[:, kp, :], f_plane_c[:, kp, :CHUNK], f_plane_c[:, kp, CHUNK:]][c]
            nc.tensor.matmul_mx(
                out=tau[piece, t],
                lhsT=j_codes[kp, g, t].bitcast(FP8X4),
                lhsT_scale=j_scales[kp, g, t],
                rhs=f_codes[kp, c][:, m0 : m0 + w].bitcast(FP8X4),
                rhs_scale=plane[:, m0 : m0 + w],
                start=(kp == 0),
                stop=(kp == PASSES - 1),
            )

        def turn_q(u):
            for h in range(2):
                bank = next_bank()
                q_banks[u, h] = bank
                for i in range(TILES):
                    if u in q_split:
                        words = q_split[u][:, i, h, :]
                    else:
                        words = q_raw[u][:, i, :].bitcast(F32)[:, h : 2 * P : 2]
                    nc.tensor.transpose(bank[:, i * P : (i + 1) * P], words, ident[:])

        def tanh_q(u, slots):
            g, c = units[u]
            for t in slots:
                tile = work.tile([P, CHUNK], F32, name="tanh%d" % t)
                tanh_t[u, t] = tile
                pairs = q_banks[u, t // 2][:].bitcast(BF16).rearrange("p (m e) -> p m e", e=2)
                nc.scalar.activation(
                    out=tile[:], in_=pairs[:, :, t % 2], func=ACT.Tanh, bias=zero_bias[:], scale=steep_col[:, g, t : t + 1]
                )

        def open_tau(piece, slots):
            bank = next_bank()
            w = piece[2]
            for e, t in enumerate(slots):
                tau[piece, t] = bank[:, e * w : (e + 1) * w]

        def multiply(piece, slots):
            open_tau(piece, slots)
            for t in slots:
                for kp in range(PASSES):
                    mx_pass(piece, t, kp)

        def finish_y(piece, t):
            u, m0, w = piece
            g, c = units[u]
            if t == 0:
                y_t[piece] = work.tile([P, PACK, w], F32, name="y_t", bufs=3)
            nc.vector.scalar_tensor_tensor(
                out=y_t[piece][:, t, :],
                in0=tanh_t[u, t][:, m0 : m0 + w],
                scalar=neg_fric_col[:, g, t : t + 1],
                in1=tau[piece, t],
                op0=ALU.mult,
                op1=ALU.add,
            )

        def turn_y(piece, slot_major):
            tiles = piece[2] // P
            for i in range(tiles):
                y_banks[piece, i] = next_bank()
            if slot_major:
                order = [(i, t) for t in range(PACK) for i in range(tiles)]
            else:
                order = [(i, t) for i in range(tiles) for t in range(PACK)]
            for i, t in order:
                nc.tensor.transpose(
                    y_banks[piece, i][:, t * P : (t + 1) * P], y_t[piece][:, t, i * P : (i + 1) * P], ident[:]
                )

        def copy_y(piece, i):
            if i == 0:
                y_rows[piece] = stage.tile([P, piece[2] // P, GROUP], F32, name="y_rows", bufs=5)
            dst = y_rows[piece][:, i, :].rearrange("m (p t) -> m p t", t=PACK)
            src = y_banks[piece, i][:].rearrange("m (t p) -> m p t", t=PACK)
            nc.scalar.copy(out=dst, in_=src)

        def store_y(piece, i0, i1, engine):
            u, m0, w = piece
            g, c = units[u]
            r0 = c * CHUNK + m0
            rows = out_0[r0 : r0 + w, g * GROUP : (g + 1) * GROUP].rearrange("(i p) n -> p i n", p=P)
            engine.dma_start(out=rows[:, i0:i1, :], in_=y_rows[piece][:, i0:i1, :])

        def round_y(piece):
            y_bf[piece] = work.tile([P, piece[2], PACK], BF16, name="y_bf", align_bytes=64)
            nc.vector.tensor_copy(
                out=y_bf[piece][:].rearrange("p (c i) t -> p c t i", i=4),
                in_=y_t[piece][:].rearrange("p t (c i) -> p c t i", i=4),
            )

        def quant_y(piece):
            u, m0, w = piece
            g, c = units[u]
            y_codes[piece] = stage.tile([P, w], U32, name="y_codes", align_bytes=64)
            nc.vector.quantize_mx(
                out=y_codes[piece][:].bitcast(FP8X4),
                scales=y_planes[g][4 * c :, m0 : m0 + w],
                in_=y_bf[piece][:].rearrange("p m t -> p (m t)"),
            )

        def store_codes(piece):
            u, m0, w = piece
            g, c = units[u]
            r0 = c * CHUNK + m0
            dst = out_1[g].rearrange("p m t -> p (m t)")[:, PACK * r0 : PACK * (r0 + w)]
            nc.sync.dma_start(out=dst.bitcast(I32), in_=y_codes[piece][:].bitcast(I32))

        def store_scales(g):
            for q in range(4):
                nc.sync.dma_start(
                    out=out_2[g, 4 * q : 4 * q + 4, :].rearrange("r (c m) -> c r m", c=CHUNKS).bitcast(I32),
                    in_=y_planes[g][32 * q : 32 * q + 4 * CHUNKS, :].bitcast(I32),
                )

        def load_f_scales(engine, plane, m0, m1):
            for r in range(4):
                engine.dma_start(
                    out=plane[r:P:32, :, :].bitcast(I32),
                    in_=f_scales[:, r:16:4, m0:m1].rearrange("g q m -> q g m").bitcast(I32),
                )

        nc.vector.memset(f_plane_a[:].bitcast(I32), 0)
        nc.vector.memset(zero_in[:], 0.0)
        nc.vector.memset(f_plane_b[:].bitcast(I32), 0)
        nc.vector.memset(f_plane_c[:].bitcast(I32), 0)
        make_identity(nc, ident[:])
        load_j(0, 0)
        load_q(0)
        nc.scalar.activation(out=zero_bias[:], in_=zero_in[:], func=ACT.Tanh)
        nc.sync.dma_start(out=steep_raw[:], in_=steep.rearrange("(g p t) -> p g t", p=P, t=PACK))
        load_f(0, [0])
        load_f_scales(nc.sync, f_plane_a, 0, CHUNK)
        load_j(1, 0)
        nc.sync.dma_start(out=fric_raw[:], in_=friction.rearrange("(g p t) -> p g t", p=P, t=PACK))
        load_j(2, 0)
        load_f(0, [1])
        load_f(0, [2])
        load_q(1)
        load_f_scales(nc.sync, f_plane_b, CHUNK, 2 * CHUNK)
        load_f(1, [0, 1, 2])
        for c in range(2, CHUNKS):
            load_j(c - 2, 1)
            load_q(c)
            if c == 2:
                load_f_scales(nc.sync, f_plane_c, 2 * CHUNK, M)
            load_f(c, [0, 1, 2])
        load_j(2, 1)
        load_q(CHUNKS)

        for kp in range(PASSES):
            group_j(kp, 0, 0)
            group_j(kp, 0, 1)
            if kp == 0:
                nc.vector.tensor_copy(out=steep_col[:], in_=steep_raw[:])
                turn_q(0)
            if kp == 1:
                nc.vector.tensor_scalar(
                    out=neg_fric_col[:], in0=fric_raw[:], scalar1=-1.0, scalar2=None, op0=ALU.mult
                )
            quant_j(kp, 0, 0)
            quant_j(kp, 0, 1)
            tanh_q(0, [[0, 1], [2], [3]][kp])
            for t in range(PACK):
                if kp == 0:
                    open_tau((0, 0, CHUNK), [t])
                mx_pass((0, 0, CHUNK), t, kp)

        def drain_rows(piece):
            u = piece[0]
            g, c = units[u]
            for i in range(TILES):
                copy_y(piece, i)
            if u + CHUNKS + 1 <= last:
                load_q(u + CHUNKS + 1)
            store_codes(piece)
            if c == CHUNKS - 1:
                store_scales(g)
            store_y(piece, 0, 2, nc.sync)
            store_y(piece, 2, TILES, nc.sync)

        first = (0, 0, CHUNK)
        for t in range(PACK):
            finish_y(first, t)
        turn_q(1)
        tanh_q(1, range(PACK))
        turn_y(first, False)

        for u in range(1, last):
            piece, before = (u, 0, CHUNK), (u - 1, 0, CHUNK)
            prep = u - 1 if u <= PASSES else None
            round_y(before)
            multiply(piece, [0])
            finish_y(piece, 0)
            quant_y(before)
            multiply(piece, [1])
            finish_y(piece, 1)
            if u > 1:
                if prep is not None:
                    group_j(prep, 1, 1)
                turn_y(before, False)
            drain_rows(before)
            if prep is None:
                split_q(u + 1)
            else:
                if u == 1:
                    group_j(prep, 1, 1)
                group_j(prep, 1, 0)
            multiply(piece, [2])
            finish_y(piece, 2)
            if prep is not None:
                quant_j(prep, 1, 0)
            multiply(piece, [3])
            finish_y(piece, 3)
            if prep is not None:
                quant_j(prep, 1, 1)
            turn_q(u + 1)
            tanh_q(u + 1, range(PACK))

        before = (last - 1, 0, CHUNK)
        pa, pb, pc = (last, 0, 2 * P), (last, 2 * P, P), (last, 3 * P, P)
        round_y(before)
        for t in range(2):
            multiply(pa, [t])
            finish_y(pa, t)
        quant_y(before)
        turn_y(before, False)
        drain_rows(before)
        for t in range(2, PACK):
            multiply(pa, [t])
            finish_y(pa, t)
        for h in range(2):
            multiply(pb, [2 * h, 2 * h + 1])
            finish_y(pb, 2 * h)
            finish_y(pb, 2 * h + 1)
        turn_y(pa, False)
        turn_y(pb, False)
        round_y(pa)
        round_y(pb)
        quant_y(pa)
        for i in range(2):
            copy_y(pa, i)
        copy_y(pb, 0)
        store_y(pa, 0, 1, nc.sync)
        store_codes(pa)
        store_y(pa, 1, 2, nc.sync)
        for t in range(PACK):
            multiply(pc, [t])
            finish_y(pc, t)
            if t == 1:
                quant_y(pb)
        store_codes(pb)
        store_y(pb, 0, 1, nc.sync)
        turn_y(pc, True)
        round_y(pc)
        quant_y(pc)
        copy_y(pc, 0)
        store_codes(pc)
        store_scales(GROUPS - 1)
        store_y(pc, 0, 1, nc.scalar)
